import numpy as np
import ml_dtypes


def mxq(x, axis, fmt="e4m3"):
    dtype, down = {"e4m3": (ml_dtypes.float8_e4m3fn, 7), "e5m2": (ml_dtypes.float8_e5m2, 14)}[fmt]
    v = np.moveaxis(np.asarray(x, np.float32).astype(ml_dtypes.bfloat16).astype(np.float64), axis, -1)
    blocks = v.reshape(v.shape[:-1] + (-1, 32))
    amax = np.abs(blocks).max(-1, keepdims=True)
    byte = np.maximum(np.where(amax > 0, np.frexp(amax)[1] - 1 + 127, 0) - down, 1)
    scale = np.exp2(byte - 127.0)
    codes = (blocks / scale).astype(np.float32).astype(dtype).astype(np.float64)
    return np.moveaxis((codes * scale).reshape(v.shape), -1, axis)


WIDE = False


def mx_kscale(k, group=512):
    if not WIDE:
        return np.ones(k)
    levels = np.array([10, -10, 5, -5, 0])
    if group != 512:
        return np.exp2(np.random.permutation(np.resize(levels, k // group))).repeat(group)
    if k % 512:
        return np.exp2(np.random.permutation(np.resize(levels, k // 32))).repeat(32)
    a = np.empty((k // 512, 16))
    for p in range(k // 512):
        a[p, :8] = np.random.permutation(np.resize(levels, 8))
        for g in range(8):
            far = levels[np.abs(levels - a[p, g]) >= 10]
            a[p, g + 8] = far[np.random.randint(len(far))]
    return np.exp2(a.ravel()).repeat(32)


def f64(x):
    return np.asarray(x).astype(np.float64)


def striped(idx):
    return np.tile(np.asarray(idx).reshape(-1, 16).T, (8, 1)).astype(np.uint16)


def unstriped(offs):
    return offs[:16].T.reshape(-1).astype(np.int64)


H, KV, D, NQ, N = 2, 2, 256, 512, 512
CAP = 2.0


def setup_inputs():
    n = np.random.standard_normal
    s = mx_kscale(D, 0)[:, None]
    u = mx_kscale(N)
    t = np.random.uniform(0.5, 2.0, N) * u
    v = n((KV, N, 128))
    return {
        "qT": (n((H, D, NQ)) * s * (0.70 / np.sqrt(D))).astype(np.float32),
        "kT": (n((KV, D, N)) / s).astype(np.float32),
        "t": t.reshape(N, 1).astype(np.float32),
        "v": (v / t[:, None]).astype(np.float32),
        "mask": (np.arange(N)[:, None] <= np.sort(np.random.randint(N // 4, N, NQ))[None, :]).astype(np.float32),
        "og": n((H, NQ, 128)).astype(np.float32),
    }


def reference(qT, kT, t, v, mask, og):
    a = mxq(f64(kT), 1, "e4m3").transpose(0, 2, 1) @ mxq(f64(qT), 1, "e4m3")
    a = CAP * np.tanh(a / CAP)
    p = np.maximum(a, 0.0)
    p = p * f64(mask)
    w = p * f64(t)
    y = mxq(w, 1, "e4m3").transpose(0, 2, 1) @ mxq(f64(v), 1, "e4m3")
    y = y / 16.0
    y = y / (1.0 + np.exp(-f64(og)))
    return y

@@ -1,0 +1,222 @@
+from contextlib import ExitStack
+
+import concourse.mybir as mybir
+
+H, D, NQ, N, E = 2, 256, 512, 512, 128
+FLOPS = 2 * H * N * NQ * D + 2 * H * NQ * N * E
+
+F32 = mybir.dt.float32
+BF16 = mybir.dt.bfloat16
+U32 = mybir.dt.uint32
+U8 = mybir.dt.uint8
+FP8X4 = mybir.dt.float8_e4m3fn_x4
+ACT = mybir.ActivationFunctionType
+ALU = mybir.AluOpType
+
+P = 128
+PACK = 4
+ROWS = D // PACK
+QC = 128
+CHUNKS = NQ // QC
+LOAD_CHUNKS = (1, 1, 2)
+K_VECTOR = 84
+
+
+def tile_rows_a_relu_mask_cap_gate_kernel(tc, qT, kT, t, v, mask, og, out):
+    nc = tc.nc
+    with ExitStack() as ctx:
+        sb = ctx.enter_context(tc.tile_pool(name="sb", bufs=1))
+        ps = ctx.enter_context(tc.psum_pool(name="ps", bufs=1))
+        ctx.enter_context(tc.manual_schedule())
+
+        k_raw = sb.tile([P, PACK, N], F32, name="k_raw")
+        nc.sync.dma_start(out=k_raw[:], in_=kT.rearrange("h (p j) n -> (h p) j n", j=PACK))
+        t_sb = sb.tile([P, PACK], F32, name="t_sb")
+        nc.scalar.dma_start(out=t_sb[:], in_=t.rearrange("(p r) one -> p (r one)", r=PACK))
+        q_rows = qT.rearrange("h (p j) n -> (h p) j n", j=PACK)
+        m_rows = mask.rearrange("(p r) n -> p r n", r=PACK)
+        q_raw, m_raw = [], []
+        c0 = 0
+        for n_chunks in LOAD_CHUNKS:
+            cols = slice(c0 * QC, (c0 + n_chunks) * QC)
+            q_tile = sb.tile([P, PACK, n_chunks * QC], F32, name="q_raw%d" % c0)
+            nc.sync.dma_start(out=q_tile[:], in_=q_rows[:, :, cols])
+            m_tile = sb.tile([P, PACK, n_chunks * QC], F32, name="m_raw%d" % c0)
+            nc.sync.dma_start(out=m_tile[:], in_=m_rows[:, :, cols])
+            for i in range(n_chunks):
+                q_raw.append(q_tile[:, :, i * QC : (i + 1) * QC])
+                m_raw.append(m_tile[:, :, i * QC : (i + 1) * QC])
+            c0 = c0 + n_chunks
+        v_raw = sb.tile([P, H, PACK, E], F32, name="v_raw")
+        nc.sync.dma_start(
+            out=v_raw[:].rearrange("p h r e -> p h (r e)"),
+            in_=v.rearrange("h (p r) e -> p h (r e)", r=PACK),
+        )
+        og_raw = []
+        for h in range(H):
+            og_tile = sb.tile([P, CHUNKS, E], F32, name="og_raw%d" % h)
+            nc.sync.dma_start(out=og_tile[:], in_=og[h].rearrange("(c p) e -> p c e", p=P))
+            og_raw.append(og_tile)
+
+        def quantize(name, src, words):
+            codes = sb.tile([P, words], U32, name=name + "_codes", align_bytes=64)
+            scales = sb.tile([P, words], U8, name=name + "_scales", align_bytes=64)
+            nc.vector.quantize_mx(out=codes[:].bitcast(FP8X4), scales=scales[:], in_=src)
+            return codes, scales
+
+        k_bf = sb.tile([P, PACK, P, PACK], BF16, name="k_bf", align_bytes=64)
+        k_dst = k_bf[:].rearrange("p r s j -> p s j r")
+        k_src = k_raw[:].rearrange("p j (s r) -> p s j r", r=PACK)
+        nc.vector.tensor_copy(out=k_dst[:, :K_VECTOR], in_=k_src[:, :K_VECTOR])
+        nc.scalar.activation(out=k_dst[:, K_VECTOR:], in_=k_src[:, K_VECTOR:], func=ACT.Copy)
+
+        t16 = sb.tile([P, PACK], F32, name="t16")
+        q_bf, q_mx, mt, score, th, w_bf, w_mx = {}, {}, {}, {}, {}, {}, {}
+
+        def cast_q(c, on_vector):
+            q_bf[c] = sb.tile([P, QC, PACK], BF16, name="q_bf%d" % c, align_bytes=64)
+            dst = q_bf[c][:].rearrange("p (a i) j -> p a j i", i=4)
+            src = q_raw[c].rearrange("p j (a i) -> p a j i", i=4)
+            if on_vector:
+                nc.vector.tensor_copy(out=dst, in_=src)
+            else:
+                nc.scalar.activation(out=dst, in_=src, func=ACT.Copy)
+
+        def quant_q(c):
+            q_mx[c] = quantize("q%d" % c, q_bf[c][:].rearrange("p n j -> p (n j)"), QC)
+
+        def make_mt(c):
+            mt[c] = sb.tile([P, QC, PACK], F32, name="mt%d" % c)
+            nc.vector.tensor_tensor(
+                out=mt[c][:].rearrange("p (a i) r -> p a r i", i=4),
+                in0=m_raw[c].rearrange("p r (a i) -> p a r i", i=4),
+                in1=t16[:].unsqueeze(1).unsqueeze(3).to_broadcast([P, QC // 4, PACK, 4]),
+                op=ALU.mult,
+            )
+
+        def scores(c):
+            for h in range(H):
+                score[c, h] = ps.tile([P, PACK, QC], F32, name="score%d" % h, bufs=2)
+            for r in range(PACK):
+                for h in range(H):
+                    rows = slice(h * ROWS, (h + 1) * ROWS)
+                    cols = slice(r * P, (r + 1) * P)
+                    nc.tensor.matmul_mx(
+                        out=score[c, h][:, r, :],
+                        lhsT=k_mx[0][rows, cols].bitcast(FP8X4),
+                        lhsT_scale=k_mx[1][rows, cols],
+                        rhs=q_mx[c][0][rows, :].bitcast(FP8X4),
+                        rhs_scale=q_mx[c][1][rows, :],
+                        start=True,
+                        stop=True,
+                    )
+
+        def cap(c, h):
+            th[c, h] = sb.tile([P, QC, PACK], F32, name="th%d%d" % (c, h))
+            nc.scalar.activation(
+                out=th[c, h][:], in_=score[c, h][:].rearrange("p r n -> p n r"), func=ACT.Tanh, scale=0.5
+            )
+
+        def weights(c, h):
+            w_bf[c, h] = sb.tile([P, QC * PACK], BF16, name="w_bf%d%d" % (c, h), align_bytes=64)
+            nc.vector.scalar_tensor_tensor(
+                out=w_bf[c, h][:],
+                in0=th[c, h][:].rearrange("p n r -> p (n r)"),
+                scalar=0.0,
+                in1=mt[c][:].rearrange("p n r -> p (n r)"),
+                op0=ALU.max,
+                op1=ALU.mult,
+            )
+
+        def quant_w(c, h):
+            w_mx[c, h] = quantize("w%d%d" % (c, h), w_bf[c, h][:], QC)
+
+        v_bf = sb.tile([P, H, E, PACK], BF16, name="v_bf", align_bytes=64)
+        gate = sb.tile([P, H, CHUNKS, E], F32, name="gate")
+
+        def cast_v(h):
+            nc.scalar.activation(
+                out=v_bf[:, h].rearrange("p (a i) r -> p a r i", i=4),
+                in_=v_raw[:, h].rearrange("p r (a i) -> p a r i", i=4),
+                func=ACT.Copy,
+            )
+
+        def make_gate(h):
+            nc.scalar.activation(out=gate[:, h], in_=og_raw[h][:], func=ACT.Tanh, scale=0.5)
+
+        y = {}
+
+        def values(c):
+            y[c] = ps.tile([P, H, E], F32, name="y%d" % c)
+            for h in range(H):
+                cols = slice(h * E, (h + 1) * E)
+                nc.tensor.matmul_mx(
+                    out=y[c][:, h, :],
+                    lhsT=w_mx[c, h][0][:].bitcast(FP8X4),
+                    lhsT_scale=w_mx[c, h][1][:],
+                    rhs=v_mx[0][:, cols].bitcast(FP8X4),
+                    rhs_scale=v_mx[1][:, cols],
+                    start=True,
+                    stop=True,
+                )
+
+        def finish(c):
+            res = sb.tile([P, H, E], F32, name="res%d" % c)
+            nc.vector.scalar_tensor_tensor(
+                out=res[:], in0=gate[:, :, c, :], scalar=1.0, in1=y[c][:], op0=ALU.add, op1=ALU.mult
+            )
+            nc.sync.dma_start(out=out[:, c * QC : (c + 1) * QC, :].rearrange("h p e -> p h e"), in_=res[:])
+
+        cast_q(0, False)
+        nc.vector.tensor_scalar(out=t16[:], in0=t_sb[:], scalar1=1.0 / 16.0, scalar2=None, op0=ALU.mult)
+        k_mx = quantize("k", k_bf[:].rearrange("p r s j -> p (r s j)"), N)
+        quant_q(0)
+        scores(0)
+        make_mt(0)
+        cast_q(1, True)
+        cap(0, 0)
+        cap(0, 1)
+        quant_q(1)
+        scores(1)
+        weights(0, 0)
+        make_mt(1)
+        weights(0, 1)
+        quant_w(0, 0)
+        cast_q(2, False)
+        cap(1, 0)
+        cap(1, 1)
+        quant_q(2)
+        scores(2)
+        quant_w(0, 1)
+        weights(1, 0)
+        cast_q(3, False)
+        weights(1, 1)
+        quant_q(3)
+        cap(2, 0)
+        cap(2, 1)
+        scores(3)
+        make_mt(2)
+        quant_w(1, 0)
+        quant_w(1, 1)
+        weights(2, 0)
+        cast_v(0)
+        cast_v(1)
+        make_mt(3)
+        weights(2, 1)
+        quant_w(2, 0)
+        v_mx = quantize("v", v_bf[:].rearrange("p h e r -> p (h e r)"), H * E)
+        cap(3, 0)
+        cap(3, 1)
+        make_gate(0)
+        make_gate(1)
+        quant_w(2, 1)
+        values(0)
+        values(1)
+        values(2)
+        weights(3, 0)
+        weights(3, 1)
+        quant_w(3, 0)
+        quant_w(3, 1)
+        values(3)
+        for c in range(CHUNKS):
+            finish(c)

@@ -18,8 +18,9 @@ PACK = 4
 ROWS = D // PACK
 QC = 128
 CHUNKS = NQ // QC
-LOAD_CHUNKS = (1, 1, 2)
-K_VECTOR = 84
+HALF = 2
+LINE = 4
+K_VECTOR = 88
 
 
 def tile_rows_a_relu_mask_cap_gate_kernel(tc, qT, kT, t, v, mask, og, out):
@@ -31,32 +32,25 @@ def tile_rows_a_relu_mask_cap_gate_kernel(tc, qT, kT, t, v, mask, og, out):
 
         k_raw = sb.tile([P, PACK, N], F32, name="k_raw")
         nc.sync.dma_start(out=k_raw[:], in_=kT.rearrange("h (p j) n -> (h p) j n", j=PACK))
-        t_sb = sb.tile([P, PACK], F32, name="t_sb")
-        nc.scalar.dma_start(out=t_sb[:], in_=t.rearrange("(p r) one -> p (r one)", r=PACK))
+        t_raw = sb.tile([P, PACK], F32, name="t_raw")
+        nc.scalar.dma_start(out=t_raw[:], in_=t.rearrange("(s r) one -> s (r one)", r=PACK))
         q_rows = qT.rearrange("h (p j) n -> (h p) j n", j=PACK)
-        m_rows = mask.rearrange("(p r) n -> p r n", r=PACK)
-        q_raw, m_raw = [], []
-        c0 = 0
-        for n_chunks in LOAD_CHUNKS:
-            cols = slice(c0 * QC, (c0 + n_chunks) * QC)
-            q_tile = sb.tile([P, PACK, n_chunks * QC], F32, name="q_raw%d" % c0)
-            nc.sync.dma_start(out=q_tile[:], in_=q_rows[:, :, cols])
-            m_tile = sb.tile([P, PACK, n_chunks * QC], F32, name="m_raw%d" % c0)
-            nc.sync.dma_start(out=m_tile[:], in_=m_rows[:, :, cols])
-            for i in range(n_chunks):
-                q_raw.append(q_tile[:, :, i * QC : (i + 1) * QC])
-                m_raw.append(m_tile[:, :, i * QC : (i + 1) * QC])
-            c0 = c0 + n_chunks
+        mask_rows = mask.rearrange("(s r) n -> s r n", r=PACK)
+        q_raw, mask_raw, og_raw = {}, {}, {}
+        for g in range(CHUNKS // HALF):
+            cols = slice(g * HALF * QC, (g + 1) * HALF * QC)
+            q_raw[g] = sb.tile([P, PACK, HALF * QC], F32, name="q_raw%d" % g)
+            nc.sync.dma_start(out=q_raw[g][:], in_=q_rows[:, :, cols])
+            mask_raw[g] = sb.tile([P, PACK, HALF * QC], F32, name="mask_raw%d" % g)
+            nc.sync.dma_start(out=mask_raw[g][:], in_=mask_rows[:, :, cols])
         v_raw = sb.tile([P, H, PACK, E], F32, name="v_raw")
         nc.sync.dma_start(
-            out=v_raw[:].rearrange("p h r e -> p h (r e)"),
-            in_=v.rearrange("h (p r) e -> p h (r e)", r=PACK),
+            out=v_raw[:].rearrange("s h r e -> s h (r e)"),
+            in_=v.rearrange("h (s r) e -> s h (r e)", r=PACK),
         )
-        og_raw = []
-        for h in range(H):
-            og_tile = sb.tile([P, CHUNKS, E], F32, name="og_raw%d" % h)
-            nc.sync.dma_start(out=og_tile[:], in_=og[h].rearrange("(c p) e -> p c e", p=P))
-            og_raw.append(og_tile)
+        for c in range(CHUNKS):
+            og_raw[c] = sb.tile([P, H, E], F32, name="og_raw%d" % c)
+            nc.sync.dma_start(out=og_raw[c][:], in_=og[:, c * QC : (c + 1) * QC, :].rearrange("h m e -> m h e"))
 
         def quantize(name, src, words):
             codes = sb.tile([P, words], U32, name=name + "_codes", align_bytes=64)
@@ -64,47 +58,57 @@ def tile_rows_a_relu_mask_cap_gate_kernel(tc, qT, kT, t, v, mask, og, out):
             nc.vector.quantize_mx(out=codes[:].bitcast(FP8X4), scales=scales[:], in_=src)
             return codes, scales
 
-        k_bf = sb.tile([P, PACK, P, PACK], BF16, name="k_bf", align_bytes=64)
-        k_dst = k_bf[:].rearrange("p r s j -> p s j r")
-        k_src = k_raw[:].rearrange("p j (s r) -> p s j r", r=PACK)
-        nc.vector.tensor_copy(out=k_dst[:, :K_VECTOR], in_=k_src[:, :K_VECTOR])
-        nc.scalar.activation(out=k_dst[:, K_VECTOR:], in_=k_src[:, K_VECTOR:], func=ACT.Copy)
-
-        t16 = sb.tile([P, PACK], F32, name="t16")
-        q_bf, q_mx, mt, score, th, w_bf, w_mx = {}, {}, {}, {}, {}, {}, {}
-
-        def cast_q(c, on_vector):
-            q_bf[c] = sb.tile([P, QC, PACK], BF16, name="q_bf%d" % c, align_bytes=64)
-            dst = q_bf[c][:].rearrange("p (a i) j -> p a j i", i=4)
-            src = q_raw[c].rearrange("p j (a i) -> p a j i", i=4)
-            if on_vector:
+        def copy_on(engine, dst, src):
+            if engine == "vector":
                 nc.vector.tensor_copy(out=dst, in_=src)
             else:
                 nc.scalar.activation(out=dst, in_=src, func=ACT.Copy)
 
-        def quant_q(c):
-            q_mx[c] = quantize("q%d" % c, q_bf[c][:].rearrange("p n j -> p (n j)"), QC)
-
-        def make_mt(c):
-            mt[c] = sb.tile([P, QC, PACK], F32, name="mt%d" % c)
-            nc.vector.tensor_tensor(
-                out=mt[c][:].rearrange("p (a i) r -> p a r i", i=4),
-                in0=m_raw[c].rearrange("p r (a i) -> p a r i", i=4),
-                in1=t16[:].unsqueeze(1).unsqueeze(3).to_broadcast([P, QC // 4, PACK, 4]),
-                op=ALU.mult,
+        def interleave(engine, dst, src):
+            copy_on(
+                engine,
+                dst.rearrange("p (a i) r -> p a r i", i=LINE),
+                src.rearrange("p r (a i) -> p a r i", i=LINE),
             )
+
+        q_bf, q_mx, mask_t, mask_t4, score, capped, w_bf, w_mx, gate, y = {}, {}, {}, {}, {}, {}, {}, {}, {}, {}
+
+        def round_q(c, engine):
+            g, i = divmod(c, HALF)
+            q_bf[c] = sb.tile([P, QC, PACK], BF16, name="q_bf%d" % c, align_bytes=64)
+            interleave(engine, q_bf[c][:], q_raw[g][:, :, i * QC : (i + 1) * QC])
+
+        def quantize_q(c):
+            q_mx[c] = quantize("q%d" % c, q_bf[c][:].rearrange("p m j -> p (m j)"), QC)
+
+        def scale_mask(g):
+            mask_t[g] = sb.tile([P, PACK, HALF * QC], F32, name="mask_t%d" % g)
+            for r in range(PACK):
+                nc.vector.tensor_scalar(
+                    out=mask_t[g][:, r, :],
+                    in0=mask_raw[g][:, r, :],
+                    scalar1=t_raw[:, r : r + 1],
+                    scalar2=1.0 / 16.0,
+                    op0=ALU.mult,
+                    op1=ALU.mult,
+                )
+
+        def interleave_mask(c, engine):
+            g, i = divmod(c, HALF)
+            mask_t4[c] = sb.tile([P, QC, PACK], F32, name="mask_t4%d" % c)
+            interleave(engine, mask_t4[c][:], mask_t[g][:, :, i * QC : (i + 1) * QC])
 
         def scores(c):
             for h in range(H):
                 score[c, h] = ps.tile([P, PACK, QC], F32, name="score%d" % h, bufs=2)
             for r in range(PACK):
+                tokens = slice(r * P, (r + 1) * P)
                 for h in range(H):
                     rows = slice(h * ROWS, (h + 1) * ROWS)
-                    cols = slice(r * P, (r + 1) * P)
                     nc.tensor.matmul_mx(
                         out=score[c, h][:, r, :],
-                        lhsT=k_mx[0][rows, cols].bitcast(FP8X4),
-                        lhsT_scale=k_mx[1][rows, cols],
+                        lhsT=k_mx[0][rows, tokens].bitcast(FP8X4),
+                        lhsT_scale=k_mx[1][rows, tokens],
                         rhs=q_mx[c][0][rows, :].bitcast(FP8X4),
                         rhs_scale=q_mx[c][1][rows, :],
                         start=True,
@@ -112,111 +116,119 @@ def tile_rows_a_relu_mask_cap_gate_kernel(tc, qT, kT, t, v, mask, og, out):
                     )
 
         def cap(c, h):
-            th[c, h] = sb.tile([P, QC, PACK], F32, name="th%d%d" % (c, h))
+            capped[c, h] = sb.tile([P, QC, PACK], F32, name="capped%d%d" % (c, h))
             nc.scalar.activation(
-                out=th[c, h][:], in_=score[c, h][:].rearrange("p r n -> p n r"), func=ACT.Tanh, scale=0.5
+                out=capped[c, h][:], in_=score[c, h][:].rearrange("s r m -> s m r"), func=ACT.Tanh, scale=0.5
             )
 
         def weights(c, h):
-            w_bf[c, h] = sb.tile([P, QC * PACK], BF16, name="w_bf%d%d" % (c, h), align_bytes=64)
+            if h == 0:
+                w_bf[c] = sb.tile([P, H, QC * PACK], BF16, name="w_bf%d" % c, align_bytes=64)
             nc.vector.scalar_tensor_tensor(
-                out=w_bf[c, h][:],
-                in0=th[c, h][:].rearrange("p n r -> p (n r)"),
+                out=w_bf[c][:, h, :],
+                in0=capped[c, h][:].rearrange("s m r -> s (m r)"),
                 scalar=0.0,
-                in1=mt[c][:].rearrange("p n r -> p (n r)"),
+                in1=mask_t4[c][:].rearrange("s m r -> s (m r)"),
                 op0=ALU.max,
                 op1=ALU.mult,
             )
 
-        def quant_w(c, h):
-            w_mx[c, h] = quantize("w%d%d" % (c, h), w_bf[c, h][:], QC)
+        def quantize_w(c, heads):
+            first, n = heads[0], len(heads)
+            src = w_bf[c][:, first : first + n, :].rearrange("s h x -> s (h x)")
+            codes, scales = quantize("w%d%d" % (c, first), src, n * QC)
+            for h in heads:
+                cols = slice((h - first) * QC, (h - first + 1) * QC)
+                w_mx[c, h] = codes[:, cols], scales[:, cols]
 
-        v_bf = sb.tile([P, H, E, PACK], BF16, name="v_bf", align_bytes=64)
-        gate = sb.tile([P, H, CHUNKS, E], F32, name="gate")
+        def make_gate(c):
+            gate[c] = sb.tile([P, H, E], F32, name="gate%d" % c)
+            nc.scalar.activation(out=gate[c][:], in_=og_raw[c][:], func=ACT.Tanh, scale=0.5)
 
-        def cast_v(h):
-            nc.scalar.activation(
-                out=v_bf[:, h].rearrange("p (a i) r -> p a r i", i=4),
-                in_=v_raw[:, h].rearrange("p r (a i) -> p a r i", i=4),
-                func=ACT.Copy,
-            )
-
-        def make_gate(h):
-            nc.scalar.activation(out=gate[:, h], in_=og_raw[h][:], func=ACT.Tanh, scale=0.5)
-
-        y = {}
-
-        def values(c):
-            y[c] = ps.tile([P, H, E], F32, name="y%d" % c)
-            for h in range(H):
+        def values(c, heads, bank):
+            acc = ps.tile([P, H, E], F32, name="y%d" % bank)
+            for h in heads:
                 cols = slice(h * E, (h + 1) * E)
                 nc.tensor.matmul_mx(
-                    out=y[c][:, h, :],
-                    lhsT=w_mx[c, h][0][:].bitcast(FP8X4),
-                    lhsT_scale=w_mx[c, h][1][:],
+                    out=acc[:, h, :],
+                    lhsT=w_mx[c, h][0].bitcast(FP8X4),
+                    lhsT_scale=w_mx[c, h][1],
                     rhs=v_mx[0][:, cols].bitcast(FP8X4),
                     rhs_scale=v_mx[1][:, cols],
                     start=True,
                     stop=True,
                 )
+            y[c, heads] = acc
 
-        def finish(c):
-            res = sb.tile([P, H, E], F32, name="res%d" % c)
+        def finish(c, heads, queue):
+            part = slice(heads[0], heads[-1] + 1)
+            res = sb.tile([P, len(heads), E], F32, name="res%d%d" % (c, heads[0]))
             nc.vector.scalar_tensor_tensor(
-                out=res[:], in0=gate[:, :, c, :], scalar=1.0, in1=y[c][:], op0=ALU.add, op1=ALU.mult
+                out=res[:], in0=gate[c][:, part, :], scalar=1.0, in1=y[c, heads][:, part, :], op0=ALU.add, op1=ALU.mult
             )
-            nc.sync.dma_start(out=out[:, c * QC : (c + 1) * QC, :].rearrange("h p e -> p h e"), in_=res[:])
+            queue.dma_start(out=out[part, c * QC : (c + 1) * QC, :].rearrange("h m e -> m h e"), in_=res[:])
 
-        cast_q(0, False)
-        nc.vector.tensor_scalar(out=t16[:], in0=t_sb[:], scalar1=1.0 / 16.0, scalar2=None, op0=ALU.mult)
+        both, first_head, second_head = (0, 1), (0,), (1,)
+
+        k_bf = sb.tile([P, PACK, P, PACK], BF16, name="k_bf", align_bytes=64)
+        k_dst = k_bf[:].rearrange("p r s j -> p s j r")
+        k_src = k_raw[:].rearrange("p j (s r) -> p s j r", r=PACK)
+        copy_on("vector", k_dst[:, :K_VECTOR], k_src[:, :K_VECTOR])
+        copy_on("scalar", k_dst[:, K_VECTOR:], k_src[:, K_VECTOR:])
+        round_q(0, "scalar")
+        round_q(1, "vector")
         k_mx = quantize("k", k_bf[:].rearrange("p r s j -> p (r s j)"), N)
-        quant_q(0)
-        scores(0)
-        make_mt(0)
-        cast_q(1, True)
+        for c in (0, 1):
+            quantize_q(c)
+            scores(c)
+        scale_mask(0)
+        interleave_mask(0, "vector")
+        interleave_mask(1, "vector")
+
         cap(0, 0)
         cap(0, 1)
-        quant_q(1)
-        scores(1)
+        round_q(2, "vector")
+        round_q(3, "scalar")
         weights(0, 0)
-        make_mt(1)
+        quantize_q(2)
+        scores(2)
         weights(0, 1)
-        quant_w(0, 0)
-        cast_q(2, False)
+        quantize_q(3)
         cap(1, 0)
         cap(1, 1)
-        quant_q(2)
-        scores(2)
-        quant_w(0, 1)
-        weights(1, 0)
-        cast_q(3, False)
-        weights(1, 1)
-        quant_q(3)
-        cap(2, 0)
-        cap(2, 1)
         scores(3)
-        make_mt(2)
-        quant_w(1, 0)
-        quant_w(1, 1)
-        weights(2, 0)
-        cast_v(0)
-        cast_v(1)
-        make_mt(3)
-        weights(2, 1)
-        quant_w(2, 0)
-        v_mx = quantize("v", v_bf[:].rearrange("p h e r -> p (h e r)"), H * E)
+        scale_mask(1)
+        weights(1, 0)
+        interleave_mask(2, "vector")
+        weights(1, 1)
+
+        v_bf = sb.tile([P, H, E, PACK], BF16, name="v_bf", align_bytes=64)
+        for h in range(H):
+            cap(2, h)
+            interleave("scalar", v_bf[:, h], v_raw[:, h])
+        interleave_mask(3, "scalar")
+        for h in range(H):
+            quantize_w(h, both)
+            weights(2, h)
         cap(3, 0)
-        cap(3, 1)
         make_gate(0)
-        make_gate(1)
-        quant_w(2, 1)
-        values(0)
-        values(1)
-        values(2)
+        cap(3, 1)
+        for c in range(1, CHUNKS):
+            make_gate(c)
+        v_mx = quantize("v", v_bf[:].rearrange("s h e r -> s (h e r)"), H * E)
+        values(0, both, 0)
+        values(1, both, 1)
+        quantize_w(2, both)
+        values(2, both, 2)
+
         weights(3, 0)
+        finish(0, both, nc.sync)
+        quantize_w(3, first_head)
+        values(3, first_head, 3)
         weights(3, 1)
-        quant_w(3, 0)
-        quant_w(3, 1)
-        values(3)
-        for c in range(CHUNKS):
-            finish(c)
+        finish(1, both, nc.sync)
+        quantize_w(3, second_head)
+        values(3, second_head, 0)
+        finish(3, first_head, nc.sync)
+        finish(2, both, nc.sync)
+        finish(3, second_head, nc.scalar)

from contextlib import ExitStack

import concourse.mybir as mybir

H, D, NQ, N, E = 2, 256, 512, 512, 128
FLOPS = 2 * H * N * NQ * D + 2 * H * NQ * N * E

F32 = mybir.dt.float32
BF16 = mybir.dt.bfloat16
U32 = mybir.dt.uint32
U8 = mybir.dt.uint8
FP8X4 = mybir.dt.float8_e4m3fn_x4
ACT = mybir.ActivationFunctionType
ALU = mybir.AluOpType

P = 128
PACK = 4
ROWS = D // PACK
QC = 128
CHUNKS = NQ // QC
HALF = 2
LINE = 4
K_VECTOR = 88


def tile_rows_a_relu_mask_cap_gate_kernel(tc, qT, kT, t, v, mask, og, out):
    nc = tc.nc
    with ExitStack() as ctx:
        sb = ctx.enter_context(tc.tile_pool(name="sb", bufs=1))
        ps = ctx.enter_context(tc.psum_pool(name="ps", bufs=1))
        ctx.enter_context(tc.manual_schedule())

        k_raw = sb.tile([P, PACK, N], F32, name="k_raw")
        nc.sync.dma_start(out=k_raw[:], in_=kT.rearrange("h (p j) n -> (h p) j n", j=PACK))
        t_raw = sb.tile([P, PACK], F32, name="t_raw")
        nc.scalar.dma_start(out=t_raw[:], in_=t.rearrange("(s r) one -> s (r one)", r=PACK))
        q_rows = qT.rearrange("h (p j) n -> (h p) j n", j=PACK)
        mask_rows = mask.rearrange("(s r) n -> s r n", r=PACK)
        q_raw, mask_raw, og_raw = {}, {}, {}
        for g in range(CHUNKS // HALF):
            cols = slice(g * HALF * QC, (g + 1) * HALF * QC)
            q_raw[g] = sb.tile([P, PACK, HALF * QC], F32, name="q_raw%d" % g)
            nc.sync.dma_start(out=q_raw[g][:], in_=q_rows[:, :, cols])
            mask_raw[g] = sb.tile([P, PACK, HALF * QC], F32, name="mask_raw%d" % g)
            nc.sync.dma_start(out=mask_raw[g][:], in_=mask_rows[:, :, cols])
        v_raw = sb.tile([P, H, PACK, E], F32, name="v_raw")
        nc.sync.dma_start(
            out=v_raw[:].rearrange("s h r e -> s h (r e)"),
            in_=v.rearrange("h (s r) e -> s h (r e)", r=PACK),
        )
        for c in range(CHUNKS):
            og_raw[c] = sb.tile([P, H, E], F32, name="og_raw%d" % c)
            nc.sync.dma_start(out=og_raw[c][:], in_=og[:, c * QC : (c + 1) * QC, :].rearrange("h m e -> m h e"))

        def quantize(name, src, words):
            codes = sb.tile([P, words], U32, name=name + "_codes", align_bytes=64)
            scales = sb.tile([P, words], U8, name=name + "_scales", align_bytes=64)
            nc.vector.quantize_mx(out=codes[:].bitcast(FP8X4), scales=scales[:], in_=src)
            return codes, scales

        def copy_on(engine, dst, src):
            if engine == "vector":
                nc.vector.tensor_copy(out=dst, in_=src)
            else:
                nc.scalar.activation(out=dst, in_=src, func=ACT.Copy)

        def interleave(engine, dst, src):
            copy_on(
                engine,
                dst.rearrange("p (a i) r -> p a r i", i=LINE),
                src.rearrange("p r (a i) -> p a r i", i=LINE),
            )

        q_bf, q_mx, mask_t, mask_t4, score, capped, w_bf, w_mx, gate, y = {}, {}, {}, {}, {}, {}, {}, {}, {}, {}

        def round_q(c, engine):
            g, i = divmod(c, HALF)
            q_bf[c] = sb.tile([P, QC, PACK], BF16, name="q_bf%d" % c, align_bytes=64)
            interleave(engine, q_bf[c][:], q_raw[g][:, :, i * QC : (i + 1) * QC])

        def quantize_q(c):
            q_mx[c] = quantize("q%d" % c, q_bf[c][:].rearrange("p m j -> p (m j)"), QC)

        def scale_mask(g):
            mask_t[g] = sb.tile([P, PACK, HALF * QC], F32, name="mask_t%d" % g)
            for r in range(PACK):
                nc.vector.tensor_scalar(
                    out=mask_t[g][:, r, :],
                    in0=mask_raw[g][:, r, :],
                    scalar1=t_raw[:, r : r + 1],
                    scalar2=1.0 / 16.0,
                    op0=ALU.mult,
                    op1=ALU.mult,
                )

        def interleave_mask(c, engine):
            g, i = divmod(c, HALF)
            mask_t4[c] = sb.tile([P, QC, PACK], F32, name="mask_t4%d" % c)
            interleave(engine, mask_t4[c][:], mask_t[g][:, :, i * QC : (i + 1) * QC])

        def scores(c):
            for h in range(H):
                score[c, h] = ps.tile([P, PACK, QC], F32, name="score%d" % h, bufs=2)
            for r in range(PACK):
                tokens = slice(r * P, (r + 1) * P)
                for h in range(H):
                    rows = slice(h * ROWS, (h + 1) * ROWS)
                    nc.tensor.matmul_mx(
                        out=score[c, h][:, r, :],
                        lhsT=k_mx[0][rows, tokens].bitcast(FP8X4),
                        lhsT_scale=k_mx[1][rows, tokens],
                        rhs=q_mx[c][0][rows, :].bitcast(FP8X4),
                        rhs_scale=q_mx[c][1][rows, :],
                        start=True,
                        stop=True,
                    )

        def cap(c, h):
            capped[c, h] = sb.tile([P, QC, PACK], F32, name="capped%d%d" % (c, h))
            nc.scalar.activation(
                out=capped[c, h][:], in_=score[c, h][:].rearrange("s r m -> s m r"), func=ACT.Tanh, scale=0.5
            )

        def weights(c, h):
            if h == 0:
                w_bf[c] = sb.tile([P, H, QC * PACK], BF16, name="w_bf%d" % c, align_bytes=64)
            nc.vector.scalar_tensor_tensor(
                out=w_bf[c][:, h, :],
                in0=capped[c, h][:].rearrange("s m r -> s (m r)"),
                scalar=0.0,
                in1=mask_t4[c][:].rearrange("s m r -> s (m r)"),
                op0=ALU.max,
                op1=ALU.mult,
            )

        def quantize_w(c, heads):
            first, n = heads[0], len(heads)
            src = w_bf[c][:, first : first + n, :].rearrange("s h x -> s (h x)")
            codes, scales = quantize("w%d%d" % (c, first), src, n * QC)
            for h in heads:
                cols = slice((h - first) * QC, (h - first + 1) * QC)
                w_mx[c, h] = codes[:, cols], scales[:, cols]

        def make_gate(c):
            gate[c] = sb.tile([P, H, E], F32, name="gate%d" % c)
            nc.scalar.activation(out=gate[c][:], in_=og_raw[c][:], func=ACT.Tanh, scale=0.5)

        def values(c, heads, bank):
            acc = ps.tile([P, H, E], F32, name="y%d" % bank)
            for h in heads:
                cols = slice(h * E, (h + 1) * E)
                nc.tensor.matmul_mx(
                    out=acc[:, h, :],
                    lhsT=w_mx[c, h][0].bitcast(FP8X4),
                    lhsT_scale=w_mx[c, h][1],
                    rhs=v_mx[0][:, cols].bitcast(FP8X4),
                    rhs_scale=v_mx[1][:, cols],
                    start=True,
                    stop=True,
                )
            y[c, heads] = acc

        def finish(c, heads, queue):
            part = slice(heads[0], heads[-1] + 1)
            res = sb.tile([P, len(heads), E], F32, name="res%d%d" % (c, heads[0]))
            nc.vector.scalar_tensor_tensor(
                out=res[:], in0=gate[c][:, part, :], scalar=1.0, in1=y[c, heads][:, part, :], op0=ALU.add, op1=ALU.mult
            )
            queue.dma_start(out=out[part, c * QC : (c + 1) * QC, :].rearrange("h m e -> m h e"), in_=res[:])

        both, first_head, second_head = (0, 1), (0,), (1,)

        k_bf = sb.tile([P, PACK, P, PACK], BF16, name="k_bf", align_bytes=64)
        k_dst = k_bf[:].rearrange("p r s j -> p s j r")
        k_src = k_raw[:].rearrange("p j (s r) -> p s j r", r=PACK)
        copy_on("vector", k_dst[:, :K_VECTOR], k_src[:, :K_VECTOR])
        copy_on("scalar", k_dst[:, K_VECTOR:], k_src[:, K_VECTOR:])
        round_q(0, "scalar")
        round_q(1, "vector")
        k_mx = quantize("k", k_bf[:].rearrange("p r s j -> p (r s j)"), N)
        for c in (0, 1):
            quantize_q(c)
            scores(c)
        scale_mask(0)
        interleave_mask(0, "vector")
        interleave_mask(1, "vector")

        cap(0, 0)
        cap(0, 1)
        round_q(2, "vector")
        round_q(3, "scalar")
        weights(0, 0)
        quantize_q(2)
        scores(2)
        weights(0, 1)
        quantize_q(3)
        cap(1, 0)
        cap(1, 1)
        scores(3)
        scale_mask(1)
        weights(1, 0)
        interleave_mask(2, "vector")
        weights(1, 1)

        v_bf = sb.tile([P, H, E, PACK], BF16, name="v_bf", align_bytes=64)
        for h in range(H):
            cap(2, h)
            interleave("scalar", v_bf[:, h], v_raw[:, h])
        interleave_mask(3, "scalar")
        for h in range(H):
            quantize_w(h, both)
            weights(2, h)
        cap(3, 0)
        make_gate(0)
        cap(3, 1)
        for c in range(1, CHUNKS):
            make_gate(c)
        v_mx = quantize("v", v_bf[:].rearrange("s h e r -> s (h e r)"), H * E)
        values(0, both, 0)
        values(1, both, 1)
        quantize_w(2, both)
        values(2, both, 2)

        weights(3, 0)
        finish(0, both, nc.sync)
        quantize_w(3, first_head)
        values(3, first_head, 3)
        weights(3, 1)
        finish(1, both, nc.sync)
        quantize_w(3, second_head)
        values(3, second_head, 0)
        finish(3, first_head, nc.sync)
        finish(2, both, nc.sync)
        finish(3, second_head, nc.scalar)
